import numpy as np
import ml_dtypes


def mxq(x, axis, fmt="e4m3"):
    dtype, down = {"e4m3": (ml_dtypes.float8_e4m3fn, 7), "e5m2": (ml_dtypes.float8_e5m2, 14)}[fmt]
    v = np.moveaxis(np.asarray(x, np.float32).astype(ml_dtypes.bfloat16).astype(np.float64), axis, -1)
    blocks = v.reshape(v.shape[:-1] + (-1, 32))
    amax = np.abs(blocks).max(-1, keepdims=True)
    byte = np.maximum(np.where(amax > 0, np.frexp(amax)[1] - 1 + 127, 0) - down, 1)
    scale = np.exp2(byte - 127.0)
    codes = (blocks / scale).astype(np.float32).astype(dtype).astype(np.float64)
    return np.moveaxis((codes * scale).reshape(v.shape), -1, axis)


WIDE = False


def mx_kscale(k):
    if not WIDE:
        return np.ones(k)
    levels = np.array([10, -10, 5, -5, 0])
    if k % 512:
        return np.exp2(np.random.permutation(np.resize(levels, k // 32))).repeat(32)
    a = np.empty((k // 512, 16))
    for p in range(k // 512):
        a[p, :8] = np.random.permutation(np.resize(levels, 8))
        for g in range(8):
            far = levels[np.abs(levels - a[p, g]) >= 10]
            a[p, g + 8] = far[np.random.randint(len(far))]
    return np.exp2(a.ravel()).repeat(32)


def f64(x):
    return np.asarray(x).astype(np.float64)


def striped(idx):
    return np.tile(idx.reshape(-1, 16).T, (8, 1)).astype(np.uint16)


def unstriped(offs):
    return offs[:16].T.reshape(-1).astype(np.int64)


def striped8(idx):
    return np.concatenate([x.reshape(-1, 16).T for x in idx]).astype(np.uint16)


def runs(offs, k):
    lists = np.stack([offs[16 * r : 16 * r + 16].T.reshape(-1) for r in range(8)]).astype(np.int64)
    return lists[np.arange(k) % 512 // 64]


def pack_weight(w):
    k, n = w.shape
    w = f64(np.asarray(w, np.float32).astype(ml_dtypes.bfloat16)).reshape(k // 32, 32, n)
    amax = np.abs(w).max(1)
    byte = np.clip(np.where(amax > 0, np.frexp(amax)[1] - 1 + 127 - 7, 1), 1, 254)
    scaled = (w * np.exp2(127.0 - byte)[:, None, :]).reshape(k, n).astype(np.float32)
    words = np.ascontiguousarray(scaled.reshape(k // 512, 128, 4, n).transpose(0, 1, 3, 2)).astype(ml_dtypes.float8_e4m3fn).view(np.uint8)
    return words, np.ascontiguousarray(byte.astype(np.uint8).reshape(k // 512, 16, n))


def unpack_weight(words, scales):
    g, p, n, _ = words.shape
    vals = np.ascontiguousarray(words).view(ml_dtypes.float8_e4m3fn).astype(np.float64) * np.repeat(np.exp2(scales.astype(np.float64) - 127.0), 8, axis=1)[..., None]
    return vals.transpose(0, 1, 3, 2).reshape(g * 512, n)


def relu(v):
    return np.maximum(v, 0.0)


K, T, S, N, G, H = 512, 2048, 512, 512, 2048, 512


def setup_inputs():
    n = np.random.standard_normal
    s = mx_kscale(K)[:, None]
    u = mx_kscale(H)
    packed_xT = pack_weight(n((K, T)) * s)
    packed_dT = pack_weight(n((K, G)) / s)
    return {
        "x_words": packed_xT[0],
        "x_scales": packed_xT[1],
        "d_words": packed_dT[0],
        "d_scales": packed_dT[1],
        "gn": (np.random.uniform(0.5, 1.5, (H, 1)) * u[:, None]).astype(np.float32),
        "w1": (n((H, H)) / np.sqrt(H) / u[:, None] * u).astype(np.float32),
        "res": (2 * n((N, S))).astype(np.float32),
        "w2": (n((H, N)) / np.sqrt(H) / u[:, None]).astype(np.float32),
        "offs": striped(np.random.permutation(T)[:S]),
        "kidx": striped8(np.random.randint(0, G, (8, H))),
        "nb": striped8(np.stack([np.random.permutation(S) for _ in range(8)])),
    }


def reference(x_words, x_scales, d_words, d_scales, gn, w1, res, w2, offs, kidx, nb):
    d_kidx = unpack_weight(d_words, d_scales)[np.arange(K)[:, None], runs(kidx, K)]
    xq = unpack_weight(x_words, x_scales)[:, unstriped(offs)]
    s = 0.0625 * (d_kidx.T @ xq)
    z = f64(gn) * s
    h = relu(mxq(f64(w1), 0, "e4m3").T @ mxq(z, 0, "e4m3"))
    z2 = h + h[np.arange(H)[:, None], runs(nb, H)]
    return f64(res) + (mxq(f64(w2), 0, "e4m3").T @ mxq(z2, 0, "e4m3"))

@@ -1,0 +1,215 @@
+from contextlib import ExitStack
+
+import concourse.mybir as mybir
+
+F32 = mybir.dt.float32
+BF16 = mybir.dt.bfloat16
+I32 = mybir.dt.int32
+U32 = mybir.dt.uint32
+U16 = mybir.dt.uint16
+U8 = mybir.dt.uint8
+FP8X4 = mybir.dt.float8_e4m3fn_x4
+ALU = mybir.AluOpType
+ACT = mybir.ActivationFunctionType
+
+P = 128
+PACK = 4
+TABLE = 2048
+S = 512
+CHUNK = 128
+CHUNKS = S // CHUNK
+HALF = 256
+FLOPS = 3 * 2 * 512 * 512 * 512
+
+
+def tile_picked_scoremlp_relu_p_kernel(
+    tc, x_words, x_scales, d_words, d_scales, gn, w1, res, w2, offs, kidx, nb, out
+):
+    nc = tc.nc
+    with ExitStack() as ctx:
+        keep = ctx.enter_context(tc.tile_pool(name="keep", bufs=1))
+        psum = ctx.enter_context(tc.psum_pool(name="psum", bufs=1))
+
+        def sb(name, shape, dtype, tag=None):
+            return keep.tile(shape, dtype, name=name, tag=tag or name, align_bytes=64)
+
+        def mx(out_ap, w_codes, w_scales, a_codes, a_scales):
+            nc.tensor.matmul_mx(
+                out=out_ap,
+                lhsT=w_codes.bitcast(FP8X4),
+                lhsT_scale=w_scales,
+                rhs=a_codes.bitcast(FP8X4),
+                rhs_scale=a_scales,
+                start=True,
+                stop=True,
+            )
+
+        def quantize(codes, scales, values):
+            nc.vector.quantize_mx(out=codes.bitcast(FP8X4), scales=scales, in_=values)
+
+        kidx_sb = sb("kidx_sb", [P, S // 16], U16)
+        offs_sb = sb("offs_sb", [P, S // 16], U16)
+        nb_sb = sb("nb_sb", [P, S // 16], U16)
+        d_scale_tab = sb("d_scale_tab", [P, TABLE], U8, "slot_a")
+        x_scale_tab = sb("x_scale_tab", [P, TABLE], U8, "slot_b")
+        d_word_tab = sb("d_word_tab", [P, TABLE], U32, "slot_c")
+        x_word_tab = sb("x_word_tab", [P, TABLE], U32, "slot_d")
+
+        nc.vector.memset(d_scale_tab[:].bitcast(I32), 0)
+        nc.gpsimd.memset(x_scale_tab[:].bitcast(I32), 0)
+        nc.sync.dma_start(kidx_sb[:], kidx)
+        nc.sync.dma_start(offs_sb[:], offs)
+        nc.sync.dma_start(nb_sb[:], nb)
+        for e in range(2):
+            nc.sync.dma_start(d_scale_tab[e:P:16, :].bitcast(I32), d_scales[0, e:16:2, :].bitcast(I32))
+        for q in range(4):
+            nc.scalar.dma_start(
+                x_scale_tab[32 * q : 32 * q + 4, :].bitcast(I32), x_scales[0, 4 * q : 4 * q + 4, :].bitcast(I32)
+            )
+        nc.sync.dma_start(d_word_tab[:].bitcast(I32), d_words[0].rearrange("p n t -> p (n t)").bitcast(I32))
+        nc.sync.dma_start(x_word_tab[:].bitcast(I32), x_words[0].rearrange("p n t -> p (n t)").bitcast(I32))
+
+
+        d_scale_got = sb("d_scale_got", [P, S], U8, "slot_e")
+        d_scale = sb("d_scale", [P, S], U8)
+        nc.vector.tensor_copy(d_scale_got[:], d_scale_tab[:].indirect(kidx_sb[:]))
+        nc.vector.tensor_copy(
+            d_scale[:].rearrange("p (t m) -> p m t", t=PACK), d_scale_got[:].rearrange("p (m t) -> p m t", t=PACK)
+        )
+        for e in range(2):
+            nc.sync.dma_start(d_scale[2 + e : P : 32, :].bitcast(I32), d_scale[16 + e : P : 32, :].bitcast(I32))
+        x_scale = sb("x_scale", [P, S], U8)
+        nc.vector.tensor_copy(x_scale[:], x_scale_tab[:].indirect(offs_sb[:]))
+        gn_sb = sb("gn_sb", [P, PACK], F32, "slot_a")
+        nc.scalar.dma_start(gn_sb[:], gn.rearrange("(p t) o -> p (t o)", t=PACK))
+        gn16 = sb("gn16", [P, PACK], F32)
+        nc.scalar.activation(gn16[:], gn_sb[:], ACT.Copy, scale=0.0625)
+        d_got = sb("d_got", [P, S], U32)
+        d_codes = sb("d_codes", [P, S], U32)
+        nc.vector.tensor_copy(d_got[:], d_word_tab[:].indirect(kidx_sb[:]))
+        nc.vector.tensor_copy(
+            d_codes[:].rearrange("p (t m) -> p m t", t=PACK), d_got[:].rearrange("p (m t) -> p m t", t=PACK)
+        )
+        x_codes = [sb("x_codes%d" % h, [P, HALF], U32) for h in range(2)]
+        for h in range(2):
+            nc.vector.tensor_copy(x_codes[h][:], x_word_tab[:].indirect(offs_sb[:, 16 * h : 16 * (h + 1)]))
+
+        w1_rows = w1.rearrange("(p t) c -> p t c", t=PACK)
+        w1_raw = [sb("w1_raw%d" % h, [P, PACK, HALF], F32, "slot_" + "eb"[h]) for h in range(2)]
+        for h in range(2):
+            nc.sync.dma_start(w1_raw[h][:], w1_rows[:, :, h * HALF : (h + 1) * HALF])
+        w2_raw = sb("w2_raw", [P, PACK, S], F32, "slot_c")
+        nc.sync.dma_start(w2_raw[:], w2.rearrange("(p t) c -> p t c", t=PACK))
+        res_sb = sb("res_sb", [P, 4, S], F32, "slot_d")
+        nc.sync.dma_start(res_sb[:], res.rearrange("(m p) j -> p m j", p=P))
+
+        w1_bf = sb("w1_bf", [P, PACK, P, PACK], BF16)
+        for h in range(2):
+            nc.scalar.copy(
+                w1_bf[:, :, 64 * h : 64 * (h + 1), :].rearrange("p u m t -> p m u t"),
+                w1_raw[h][:].rearrange("p t (m u) -> p m u t", u=PACK),
+            )
+        w1_codes = sb("w1_codes", [P, S], U32)
+        w1_scale = sb("w1_scale", [P, S], U8)
+
+        s_bank = [psum.tile([P, PACK, CHUNK], F32, name="s_bank%d" % c, tag="a%d" % c) for c in range(CHUNKS)]
+        for c in range(CHUNKS):
+            cols = slice(c % 2 * CHUNK, (c % 2 + 1) * CHUNK)
+            for t in range(PACK):
+                rows = slice(t * P, (t + 1) * P)
+                mx(s_bank[c][:, t, :], d_codes[:, rows], d_scale[:, rows], x_codes[c // 2][:, cols],
+                   x_scale[:, c * CHUNK : (c + 1) * CHUNK])
+        z_bf = [sb("z_bf%d" % c, [P, CHUNK, PACK], BF16) for c in range(CHUNKS)]
+        z_codes = [sb("z_codes%d" % c, [P, CHUNK], U32) for c in range(CHUNKS)]
+        z_scale = [sb("z_scale%d" % c, [P, CHUNK], U8) for c in range(CHUNKS)]
+        gn_spread = gn16[:].unsqueeze(1).to_broadcast([P, CHUNK, PACK])
+
+        def weigh(c):
+            nc.vector.tensor_tensor(z_bf[c][:], s_bank[c][:].rearrange("p t n -> p n t"), gn_spread, ALU.mult)
+
+        def quantize_z(c):
+            quantize(z_codes[c][:], z_scale[c][:], z_bf[c][:].rearrange("p n t -> p (n t)"))
+
+        weigh(0)
+        weigh(1)
+        quantize_z(0)
+        quantize(w1_codes[:], w1_scale[:], w1_bf[:].rearrange("p u m t -> p (u m t)"))
+        for c in range(2, CHUNKS):
+            quantize_z(c - 1)
+            weigh(c)
+        quantize_z(CHUNKS - 1)
+
+        h_bank = [psum.tile([P, PACK, CHUNK], F32, name="h_bank%d" % c, tag="b%d" % c) for c in range(CHUNKS)]
+        h_plane = [sb("h_plane%d" % u, [P, S], F32) for u in range(PACK)]
+        for c in range(CHUNKS):
+            for u in range(PACK):
+                rows = slice(u * P, (u + 1) * P)
+                mx(h_bank[c][:, u, :], w1_codes[:, rows], w1_scale[:, rows], z_codes[c][:], z_scale[c][:])
+            for u in range(PACK):
+                h_cols = h_plane[u][:, c * CHUNK : (c + 1) * CHUNK]
+                if c < CHUNKS - 1:
+                    nc.scalar.activation(h_cols, h_bank[c][:, u, :], ACT.Relu)
+                else:
+                    nc.vector.tensor_scalar_max(h_cols, h_bank[c][:, u, :], 0.0)
+
+        w2_bf = sb("w2_bf", [P, S, PACK], BF16)
+        for h in range(2):
+            cols = slice(h * HALF, (h + 1) * HALF)
+            nc.scalar.copy(
+                w2_bf[:, cols, :].rearrange("p (c i) t -> p c t i", i=4),
+                w2_raw[:, :, cols].rearrange("p t (c i) -> p c t i", i=4),
+            )
+        w2_codes = sb("w2_codes", [P, S], U32)
+        w2_scale = sb("w2_scale", [P, S], U8)
+
+        near = [sb("near%d" % h, [P, PACK, HALF], F32) for h in range(2)]
+        z2_bf = [sb("z2_bf%d" % c, [P, CHUNK, PACK], BF16) for c in range(CHUNKS)]
+        z2_codes = [sb("z2_codes%d" % c, [P, CHUNK], U32) for c in range(CHUNKS)]
+        z2_scale = [sb("z2_scale%d" % c, [P, CHUNK], U8) for c in range(CHUNKS)]
+        out_view = out.rearrange("(m p) j -> p m j", p=P)
+        y_bank = {}
+
+        def fetch(h):
+            for u in range(PACK):
+                nc.vector.tensor_copy(near[h][:, u, :], h_plane[u][:].indirect(nb_sb[:, 16 * h : 16 * (h + 1)]))
+
+        def join(c):
+            cols = slice(c % 2 * CHUNK, (c % 2 + 1) * CHUNK)
+            nc.vector.scalar_tensor_tensor(
+                z2_bf[c][:],
+                h_bank[c][:].rearrange("p u n -> p n u"),
+                0.0,
+                near[c // 2][:, :, cols].rearrange("p u n -> p n u"),
+                ALU.max,
+                ALU.add,
+            )
+
+        def last_layer(c):
+            quantize(z2_codes[c][:], z2_scale[c][:], z2_bf[c][:].rearrange("p n t -> p (n t)"))
+            y_bank[c] = psum.tile([P, 4, CHUNK], F32, name="y_bank%d" % c, tag="a%d" % c)
+            for m in range(4):
+                rows = slice(m * P, (m + 1) * P)
+                mx(y_bank[c][:, m, :], w2_codes[:, rows], w2_scale[:, rows], z2_codes[c][:], z2_scale[c][:])
+
+        def finish(c):
+            cols = slice(c * CHUNK, (c + 1) * CHUNK)
+            y = sb("y%d" % c, [P, 4, CHUNK], F32)
+            nc.vector.tensor_tensor(y[:], y_bank[c][:], res_sb[:, :, cols], ALU.add)
+            nc.sync.dma_start(out_view[:, 0:2, cols], y[:, 0:2, :])
+            nc.scalar.dma_start(out_view[:, 2:4, cols], y[:, 2:4, :])
+
+        fetch(0)
+        quantize(w2_codes[:], w2_scale[:], w2_bf[:].rearrange("p c t -> p (c t)"))
+        join(0)
+        join(1)
+        last_layer(0)
+        last_layer(1)
+        fetch(1)
+        join(2)
+        finish(0)
+        join(3)
+        last_layer(2)
+        finish(1)
+        last_layer(3)
+        finish(2)
+        finish(3)

@@ -74,21 +74,22 @@ def tile_picked_scoremlp_relu_p_kernel(
         d_scale = sb("d_scale", [P, S], U8)
         nc.vector.tensor_copy(d_scale_got[:], d_scale_tab[:].indirect(kidx_sb[:]))
         nc.vector.tensor_copy(
-            d_scale[:].rearrange("p (t m) -> p m t", t=PACK), d_scale_got[:].rearrange("p (m t) -> p m t", t=PACK)
+            d_scale[:].rearrange("p (t m) -> p t m", t=PACK), d_scale_got[:].rearrange("p (m t) -> p t m", t=PACK)
         )
         for e in range(2):
             nc.sync.dma_start(d_scale[2 + e : P : 32, :].bitcast(I32), d_scale[16 + e : P : 32, :].bitcast(I32))
         x_scale = sb("x_scale", [P, S], U8)
         nc.vector.tensor_copy(x_scale[:], x_scale_tab[:].indirect(offs_sb[:]))
-        gn_sb = sb("gn_sb", [P, PACK], F32, "slot_a")
-        nc.scalar.dma_start(gn_sb[:], gn.rearrange("(p t) o -> p (t o)", t=PACK))
+        gn_sb = sb("gn_sb", [P, PACK], F32)
+        nc.gpsimd.dma_start(gn_sb[:], gn.rearrange("(p t) o -> p (t o)", t=PACK))
         gn16 = sb("gn16", [P, PACK], F32)
         nc.scalar.activation(gn16[:], gn_sb[:], ACT.Copy, scale=0.0625)
         d_got = sb("d_got", [P, S], U32)
         d_codes = sb("d_codes", [P, S], U32)
         nc.vector.tensor_copy(d_got[:], d_word_tab[:].indirect(kidx_sb[:]))
         nc.vector.tensor_copy(
-            d_codes[:].rearrange("p (t m) -> p m t", t=PACK), d_got[:].rearrange("p (m t) -> p m t", t=PACK)
+            d_codes[:].rearrange("p (t g i) -> p g t i", t=PACK, i=4),
+            d_got[:].rearrange("p (g i t) -> p g t i", t=PACK, i=4),
         )
         x_codes = [sb("x_codes%d" % h, [P, HALF], U32) for h in range(2)]
         for h in range(2):
@@ -98,10 +99,8 @@ def tile_picked_scoremlp_relu_p_kernel(
         w1_raw = [sb("w1_raw%d" % h, [P, PACK, HALF], F32, "slot_" + "eb"[h]) for h in range(2)]
         for h in range(2):
             nc.sync.dma_start(w1_raw[h][:], w1_rows[:, :, h * HALF : (h + 1) * HALF])
-        w2_raw = sb("w2_raw", [P, PACK, S], F32, "slot_c")
+        w2_raw = sb("w2_raw", [P, PACK, S], F32, "slot_d")
         nc.sync.dma_start(w2_raw[:], w2.rearrange("(p t) c -> p t c", t=PACK))
-        res_sb = sb("res_sb", [P, 4, S], F32, "slot_d")
-        nc.sync.dma_start(res_sb[:], res.rearrange("(m p) j -> p m j", p=P))
 
         w1_bf = sb("w1_bf", [P, PACK, P, PACK], BF16)
         for h in range(2):
@@ -112,49 +111,68 @@ def tile_picked_scoremlp_relu_p_kernel(
         w1_codes = sb("w1_codes", [P, S], U32)
         w1_scale = sb("w1_scale", [P, S], U8)
 
-        s_bank = [psum.tile([P, PACK, CHUNK], F32, name="s_bank%d" % c, tag="a%d" % c) for c in range(CHUNKS)]
-        for c in range(CHUNKS):
-            cols = slice(c % 2 * CHUNK, (c % 2 + 1) * CHUNK)
+        s_bank = [psum.tile([P, PACK, CHUNK], F32, name="s_bank%d" % c, tag="a%d" % c) for c in range(2)]
+        for c in range(2):
+            cols = slice(c * CHUNK, (c + 1) * CHUNK)
             for t in range(PACK):
                 rows = slice(t * P, (t + 1) * P)
-                mx(s_bank[c][:, t, :], d_codes[:, rows], d_scale[:, rows], x_codes[c // 2][:, cols],
-                   x_scale[:, c * CHUNK : (c + 1) * CHUNK])
-        z_bf = [sb("z_bf%d" % c, [P, CHUNK, PACK], BF16) for c in range(CHUNKS)]
-        z_codes = [sb("z_codes%d" % c, [P, CHUNK], U32) for c in range(CHUNKS)]
-        z_scale = [sb("z_scale%d" % c, [P, CHUNK], U8) for c in range(CHUNKS)]
+                mx(s_bank[c][:, t, :], d_codes[:, rows], d_scale[:, rows], x_codes[0][:, cols], x_scale[:, cols])
+        s_pair = [psum.tile([P, 2, HALF], F32, name="s_pair%d" % b, tag="a%d" % (2 + b)) for b in range(2)]
+        z_planes = sb("z_planes", [P, PACK, HALF], BF16, "slot_b")
+        for t in range(PACK):
+            rows = slice(t * P, (t + 1) * P)
+            mx(s_pair[t // 2][:, t % 2, :], d_codes[:, rows], d_scale[:, rows], x_codes[1][:], x_scale[:, HALF:S])
+        for t in range(PACK):
+            nc.scalar.activation(z_planes[:, t, :], s_pair[t // 2][:, t % 2, :], ACT.Copy, scale=gn16[:, t : t + 1])
+        z_bf = [sb("z_bf%d" % h, [P, HALF, PACK], BF16, "slot_y%d" % h) for h in range(2)]
+        z_codes = [sb("z_codes%d" % h, [P, HALF], U32) for h in range(2)]
+        z_scale = [sb("z_scale%d" % h, [P, HALF], U8) for h in range(2)]
         gn_spread = gn16[:].unsqueeze(1).to_broadcast([P, CHUNK, PACK])
 
         def weigh(c):
-            nc.vector.tensor_tensor(z_bf[c][:], s_bank[c][:].rearrange("p t n -> p n t"), gn_spread, ALU.mult)
+            cols = slice(c % 2 * CHUNK, (c % 2 + 1) * CHUNK)
+            nc.vector.tensor_tensor(
+                z_bf[c // 2][:, cols, :], s_bank[c][:].rearrange("p t n -> p n t"), gn_spread, ALU.mult
+            )
 
-        def quantize_z(c):
-            quantize(z_codes[c][:], z_scale[c][:], z_bf[c][:].rearrange("p n t -> p (n t)"))
+        def quantize_z(h):
+            quantize(z_codes[h][:], z_scale[h][:], z_bf[h][:].rearrange("p n t -> p (n t)"))
 
         weigh(0)
         weigh(1)
-        quantize_z(0)
         quantize(w1_codes[:], w1_scale[:], w1_bf[:].rearrange("p u m t -> p (u m t)"))
-        for c in range(2, CHUNKS):
-            quantize_z(c - 1)
-            weigh(c)
-        quantize_z(CHUNKS - 1)
+        quantize_z(0)
+        nc.vector.tensor_copy(
+            z_bf[1][:].rearrange("p (g i) t -> p g t i", i=4), z_planes[:].rearrange("p t (g i) -> p g t i", i=4)
+        )
+        quantize_z(1)
 
-        h_bank = [psum.tile([P, PACK, CHUNK], F32, name="h_bank%d" % c, tag="b%d" % c) for c in range(CHUNKS)]
+        res_sb = sb("res_sb", [P, 4, S], F32, "slot_b")
+        nc.sync.dma_start(res_sb[:], res.rearrange("(m p) j -> p m j", p=P))
+
+        h_own = [sb("h_own%d" % h, [P, PACK, HALF], F32) for h in range(2)]
         h_plane = [sb("h_plane%d" % u, [P, S], F32) for u in range(PACK)]
-        for c in range(CHUNKS):
+        h_bank = [
+            [psum.tile([P, 2, HALF], F32, name="h_bank%d%d" % (h, b), tag="b%d%d" % (h, b)) for b in range(2)]
+            for h in range(2)
+        ]
+        for h in range(2):
             for u in range(PACK):
                 rows = slice(u * P, (u + 1) * P)
-                mx(h_bank[c][:, u, :], w1_codes[:, rows], w1_scale[:, rows], z_codes[c][:], z_scale[c][:])
-            for u in range(PACK):
-                h_cols = h_plane[u][:, c * CHUNK : (c + 1) * CHUNK]
-                if c < CHUNKS - 1:
-                    nc.scalar.activation(h_cols, h_bank[c][:, u, :], ACT.Relu)
-                else:
-                    nc.vector.tensor_scalar_max(h_cols, h_bank[c][:, u, :], 0.0)
+                mx(h_bank[h][u // 2][:, u % 2, :], w1_codes[:, rows], w1_scale[:, rows], z_codes[h][:], z_scale[h][:])
+        for u in range(PACK):
+            nc.scalar.activation(h_plane[u][:, 0:HALF], h_bank[0][u // 2][:, u % 2, :], ACT.Relu)
+        nc.vector.tensor_scalar_max(h_own[0][:, 0:2, :], h_bank[0][0][:], 0.0)
+        nc.vector.tensor_scalar_max(h_plane[0][:, HALF:S], h_bank[1][0][:, 0, :], 0.0)
+        nc.scalar.activation(h_own[0][:, 2:4, :], h_bank[0][1][:], ACT.Relu)
+        for u in range(1, PACK):
+            nc.scalar.activation(h_plane[u][:, HALF:S], h_bank[1][u // 2][:, u % 2, :], ACT.Relu)
+        for b in range(2):
+            nc.scalar.activation(h_own[1][:, 2 * b : 2 * b + 2, :], h_bank[1][b][:], ACT.Relu)
 
-        w2_bf = sb("w2_bf", [P, S, PACK], BF16)
-        for h in range(2):
-            cols = slice(h * HALF, (h + 1) * HALF)
+        w2_bf = sb("w2_bf", [P, S, PACK], BF16, "slot_y1")
+        for c in range(CHUNKS):
+            cols = slice(c * CHUNK, (c + 1) * CHUNK)
             nc.scalar.copy(
                 w2_bf[:, cols, :].rearrange("p (c i) t -> p c t i", i=4),
                 w2_raw[:, :, cols].rearrange("p t (c i) -> p c t i", i=4),
@@ -162,54 +180,56 @@ def tile_picked_scoremlp_relu_p_kernel(
         w2_codes = sb("w2_codes", [P, S], U32)
         w2_scale = sb("w2_scale", [P, S], U8)
 
-        near = [sb("near%d" % h, [P, PACK, HALF], F32) for h in range(2)]
-        z2_bf = [sb("z2_bf%d" % c, [P, CHUNK, PACK], BF16) for c in range(CHUNKS)]
-        z2_codes = [sb("z2_codes%d" % c, [P, CHUNK], U32) for c in range(CHUNKS)]
-        z2_scale = [sb("z2_scale%d" % c, [P, CHUNK], U8) for c in range(CHUNKS)]
         out_view = out.rearrange("(m p) j -> p m j", p=P)
-        y_bank = {}
+        pieces = [(0, 256), (256, 384), (384, 512)]
+        z2_bf, y_bank = {}, {}
 
-        def fetch(h):
+        def join(k, slot=None):
+            first, last = pieces[k]
+            width = last - first
+            z2 = sb("z2_%d" % k, [P, PACK, width], F32, slot)
+            own = h_own[first // HALF][:, :, first % HALF : first % HALF + width]
             for u in range(PACK):
-                nc.vector.tensor_copy(near[h][:, u, :], h_plane[u][:].indirect(nb_sb[:, 16 * h : 16 * (h + 1)]))
-
-        def join(c):
-            cols = slice(c % 2 * CHUNK, (c % 2 + 1) * CHUNK)
-            nc.vector.scalar_tensor_tensor(
-                z2_bf[c][:],
-                h_bank[c][:].rearrange("p u n -> p n u"),
-                0.0,
-                near[c // 2][:, :, cols].rearrange("p u n -> p n u"),
-                ALU.max,
-                ALU.add,
+                picked = h_plane[u][:].indirect(nb_sb[:, first // 16 : last // 16])
+                nc.vector.tensor_tensor(z2[:, u, :], picked, own[:, u, :], ALU.add)
+            z2_bf[k] = sb("z2_bf%d" % k, [P, width, PACK], BF16, "slot_z%d" % k)
+            nc.scalar.copy(
+                z2_bf[k][:].rearrange("p (g i) u -> p g u i", i=4), z2[:].rearrange("p u (g i) -> p g u i", i=4)
             )
 
-        def last_layer(c):
-            quantize(z2_codes[c][:], z2_scale[c][:], z2_bf[c][:].rearrange("p n t -> p (n t)"))
-            y_bank[c] = psum.tile([P, 4, CHUNK], F32, name="y_bank%d" % c, tag="a%d" % c)
-            for m in range(4):
-                rows = slice(m * P, (m + 1) * P)
-                mx(y_bank[c][:, m, :], w2_codes[:, rows], w2_scale[:, rows], z2_codes[c][:], z2_scale[c][:])
+        def last_layer(k):
+            first, last = pieces[k]
+            width = last - first
+            codes = sb("z2_codes%d" % k, [P, width], U32)
+            scale = sb("z2_scale%d" % k, [P, width], U8)
+            quantize(codes[:], scale[:], z2_bf[k][:].rearrange("p n t -> p (n t)"))
+            per_bank = S // width
+            for b in range(4 // per_bank):
+                tag = "a%d" % (first // CHUNK + b)
+                y_bank[k, b] = psum.tile([P, per_bank, width], F32, name="y_bank%d%d" % (k, b), tag=tag)
+                for i in range(per_bank):
+                    rows = slice((b * per_bank + i) * P, (b * per_bank + i + 1) * P)
+                    mx(y_bank[k, b][:, i, :], w2_codes[:, rows], w2_scale[:, rows], codes[:], scale[:])
 
-        def finish(c):
-            cols = slice(c * CHUNK, (c + 1) * CHUNK)
-            y = sb("y%d" % c, [P, 4, CHUNK], F32)
-            nc.vector.tensor_tensor(y[:], y_bank[c][:], res_sb[:, :, cols], ALU.add)
-            nc.sync.dma_start(out_view[:, 0:2, cols], y[:, 0:2, :])
-            nc.scalar.dma_start(out_view[:, 2:4, cols], y[:, 2:4, :])
+        def finish(k, b):
+            first, last = pieces[k]
+            width = last - first
+            per_bank = S // width
+            half = per_bank // 2
+            y = sb("y%d%d" % (k, b), [P, per_bank, width], F32)
+            lo = b * per_bank
+            nc.vector.tensor_tensor(y[:], y_bank[k, b][:], res_sb[:, lo : lo + per_bank, first:last], ALU.add)
+            nc.sync.dma_start(out_view[:, lo : lo + half, first:last], y[:, 0:half, :])
+            nc.scalar.dma_start(out_view[:, lo + half : lo + per_bank, first:last], y[:, half:per_bank, :])
 
-        fetch(0)
-        quantize(w2_codes[:], w2_scale[:], w2_bf[:].rearrange("p c t -> p (c t)"))
         join(0)
         join(1)
+        quantize(w2_codes[:], w2_scale[:], w2_bf[:].rearrange("p c t -> p (c t)"))
         last_layer(0)
+        join(2, "slot_z0")
         last_layer(1)
-        fetch(1)
-        join(2)
-        finish(0)
-        join(3)
+        finish(0, 0)
         last_layer(2)
-        finish(1)
-        last_layer(3)
-        finish(2)
-        finish(3)
+        finish(0, 1)
+        finish(1, 0)
+        finish(2, 0)

@@ -102,7 +102,7 @@ def tile_picked_scoremlp_relu_p_kernel(
         w2_raw = sb("w2_raw", [P, PACK, S], F32, "slot_d")
         nc.sync.dma_start(w2_raw[:], w2.rearrange("(p t) c -> p t c", t=PACK))
 
-        w1_bf = sb("w1_bf", [P, PACK, P, PACK], BF16)
+        w1_bf = sb("w1_bf", [P, PACK, P, PACK], BF16, "slot_w")
         for h in range(2):
             nc.scalar.copy(
                 w1_bf[:, :, 64 * h : 64 * (h + 1), :].rearrange("p u m t -> p m u t"),
@@ -111,21 +111,18 @@ def tile_picked_scoremlp_relu_p_kernel(
         w1_codes = sb("w1_codes", [P, S], U32)
         w1_scale = sb("w1_scale", [P, S], U8)
 
-        s_bank = [psum.tile([P, PACK, CHUNK], F32, name="s_bank%d" % c, tag="a%d" % c) for c in range(2)]
-        for c in range(2):
-            cols = slice(c * CHUNK, (c + 1) * CHUNK)
+        s_bank = [psum.tile([P, PACK, CHUNK], F32, name="s_bank%d" % c, tag="a%d" % c) for c in range(CHUNKS)]
+        for c in (0, 1, 3, 2):
+            cols = slice(c % 2 * CHUNK, (c % 2 + 1) * CHUNK)
             for t in range(PACK):
                 rows = slice(t * P, (t + 1) * P)
-                mx(s_bank[c][:, t, :], d_codes[:, rows], d_scale[:, rows], x_codes[0][:, cols], x_scale[:, cols])
-        s_pair = [psum.tile([P, 2, HALF], F32, name="s_pair%d" % b, tag="a%d" % (2 + b)) for b in range(2)]
-        z_planes = sb("z_planes", [P, PACK, HALF], BF16, "slot_b")
+                mx(s_bank[c][:, t, :], d_codes[:, rows], d_scale[:, rows], x_codes[c // 2][:, cols],
+                   x_scale[:, c * CHUNK : (c + 1) * CHUNK])
+        z_planes = sb("z_planes", [P, PACK, CHUNK], BF16, "slot_b")
         for t in range(PACK):
-            rows = slice(t * P, (t + 1) * P)
-            mx(s_pair[t // 2][:, t % 2, :], d_codes[:, rows], d_scale[:, rows], x_codes[1][:], x_scale[:, HALF:S])
-        for t in range(PACK):
-            nc.scalar.activation(z_planes[:, t, :], s_pair[t // 2][:, t % 2, :], ACT.Copy, scale=gn16[:, t : t + 1])
-        z_bf = [sb("z_bf%d" % h, [P, HALF, PACK], BF16, "slot_y%d" % h) for h in range(2)]
-        z_codes = [sb("z_codes%d" % h, [P, HALF], U32) for h in range(2)]
+            nc.scalar.activation(z_planes[:, t, :], s_bank[3][:, t, :], ACT.Copy, scale=gn16[:, t : t + 1])
+        z_bf = [sb("z_bf%d" % h, [P, HALF, PACK], BF16) for h in range(2)]
+        z_codes = [sb("z_codes%d" % h, [P, HALF], U32, "slot_y%d" % h) for h in range(2)]
         z_scale = [sb("z_scale%d" % h, [P, HALF], U8) for h in range(2)]
         gn_spread = gn16[:].unsqueeze(1).to_broadcast([P, CHUNK, PACK])
 
@@ -143,8 +140,10 @@ def tile_picked_scoremlp_relu_p_kernel(
         quantize(w1_codes[:], w1_scale[:], w1_bf[:].rearrange("p u m t -> p (u m t)"))
         quantize_z(0)
         nc.vector.tensor_copy(
-            z_bf[1][:].rearrange("p (g i) t -> p g t i", i=4), z_planes[:].rearrange("p t (g i) -> p g t i", i=4)
+            z_bf[1][:, CHUNK:HALF, :].rearrange("p (g i) t -> p g t i", i=4),
+            z_planes[:].rearrange("p t (g i) -> p g t i", i=4),
         )
+        weigh(2)
         quantize_z(1)
 
         res_sb = sb("res_sb", [P, 4, S], F32, "slot_b")
@@ -170,12 +169,11 @@ def tile_picked_scoremlp_relu_p_kernel(
         for b in range(2):
             nc.scalar.activation(h_own[1][:, 2 * b : 2 * b + 2, :], h_bank[1][b][:], ACT.Relu)
 
-        w2_bf = sb("w2_bf", [P, S, PACK], BF16, "slot_y1")
+        w2_bf = [sb("w2_bf%d" % h, [P, HALF, PACK], BF16, ("slot_w", "slot_y1")[h]) for h in range(2)]
         for c in range(CHUNKS):
-            cols = slice(c * CHUNK, (c + 1) * CHUNK)
             nc.scalar.copy(
-                w2_bf[:, cols, :].rearrange("p (c i) t -> p c t i", i=4),
-                w2_raw[:, :, cols].rearrange("p t (c i) -> p c t i", i=4),
+                w2_bf[c // 2][:, c % 2 * CHUNK : (c % 2 + 1) * CHUNK, :].rearrange("p (c i) t -> p c t i", i=4),
+                w2_raw[:, :, c * CHUNK : (c + 1) * CHUNK].rearrange("p t (c i) -> p c t i", i=4),
             )
         w2_codes = sb("w2_codes", [P, S], U32)
         w2_scale = sb("w2_scale", [P, S], U8)
@@ -224,7 +222,9 @@ def tile_picked_scoremlp_relu_p_kernel(
 
         join(0)
         join(1)
-        quantize(w2_codes[:], w2_scale[:], w2_bf[:].rearrange("p c t -> p (c t)"))
+        for h in range(2):
+            cols = slice(h * HALF, (h + 1) * HALF)
+            quantize(w2_codes[:, cols], w2_scale[:, cols], w2_bf[h][:].rearrange("p c t -> p (c t)"))
         last_layer(0)
         join(2, "slot_z0")
         last_layer(1)

from contextlib import ExitStack

import concourse.mybir as mybir

F32 = mybir.dt.float32
BF16 = mybir.dt.bfloat16
I32 = mybir.dt.int32
U32 = mybir.dt.uint32
U16 = mybir.dt.uint16
U8 = mybir.dt.uint8
FP8X4 = mybir.dt.float8_e4m3fn_x4
ALU = mybir.AluOpType
ACT = mybir.ActivationFunctionType

P = 128
PACK = 4
TABLE = 2048
S = 512
CHUNK = 128
CHUNKS = S // CHUNK
HALF = 256
FLOPS = 3 * 2 * 512 * 512 * 512


def tile_picked_scoremlp_relu_p_kernel(
    tc, x_words, x_scales, d_words, d_scales, gn, w1, res, w2, offs, kidx, nb, out
):
    nc = tc.nc
    with ExitStack() as ctx:
        keep = ctx.enter_context(tc.tile_pool(name="keep", bufs=1))
        psum = ctx.enter_context(tc.psum_pool(name="psum", bufs=1))

        def sb(name, shape, dtype, tag=None):
            return keep.tile(shape, dtype, name=name, tag=tag or name, align_bytes=64)

        def mx(out_ap, w_codes, w_scales, a_codes, a_scales):
            nc.tensor.matmul_mx(
                out=out_ap,
                lhsT=w_codes.bitcast(FP8X4),
                lhsT_scale=w_scales,
                rhs=a_codes.bitcast(FP8X4),
                rhs_scale=a_scales,
                start=True,
                stop=True,
            )

        def quantize(codes, scales, values):
            nc.vector.quantize_mx(out=codes.bitcast(FP8X4), scales=scales, in_=values)

        kidx_sb = sb("kidx_sb", [P, S // 16], U16)
        offs_sb = sb("offs_sb", [P, S // 16], U16)
        nb_sb = sb("nb_sb", [P, S // 16], U16)
        d_scale_tab = sb("d_scale_tab", [P, TABLE], U8, "slot_a")
        x_scale_tab = sb("x_scale_tab", [P, TABLE], U8, "slot_b")
        d_word_tab = sb("d_word_tab", [P, TABLE], U32, "slot_c")
        x_word_tab = sb("x_word_tab", [P, TABLE], U32, "slot_d")

        nc.vector.memset(d_scale_tab[:].bitcast(I32), 0)
        nc.gpsimd.memset(x_scale_tab[:].bitcast(I32), 0)
        nc.sync.dma_start(kidx_sb[:], kidx)
        nc.sync.dma_start(offs_sb[:], offs)
        nc.sync.dma_start(nb_sb[:], nb)
        for e in range(2):
            nc.sync.dma_start(d_scale_tab[e:P:16, :].bitcast(I32), d_scales[0, e:16:2, :].bitcast(I32))
        for q in range(4):
            nc.scalar.dma_start(
                x_scale_tab[32 * q : 32 * q + 4, :].bitcast(I32), x_scales[0, 4 * q : 4 * q + 4, :].bitcast(I32)
            )
        nc.sync.dma_start(d_word_tab[:].bitcast(I32), d_words[0].rearrange("p n t -> p (n t)").bitcast(I32))
        nc.sync.dma_start(x_word_tab[:].bitcast(I32), x_words[0].rearrange("p n t -> p (n t)").bitcast(I32))


        d_scale_got = sb("d_scale_got", [P, S], U8, "slot_e")
        d_scale = sb("d_scale", [P, S], U8)
        nc.vector.tensor_copy(d_scale_got[:], d_scale_tab[:].indirect(kidx_sb[:]))
        nc.vector.tensor_copy(
            d_scale[:].rearrange("p (t m) -> p t m", t=PACK), d_scale_got[:].rearrange("p (m t) -> p t m", t=PACK)
        )
        for e in range(2):
            nc.sync.dma_start(d_scale[2 + e : P : 32, :].bitcast(I32), d_scale[16 + e : P : 32, :].bitcast(I32))
        x_scale = sb("x_scale", [P, S], U8)
        nc.vector.tensor_copy(x_scale[:], x_scale_tab[:].indirect(offs_sb[:]))
        gn_sb = sb("gn_sb", [P, PACK], F32)
        nc.gpsimd.dma_start(gn_sb[:], gn.rearrange("(p t) o -> p (t o)", t=PACK))
        gn16 = sb("gn16", [P, PACK], F32)
        nc.scalar.activation(gn16[:], gn_sb[:], ACT.Copy, scale=0.0625)
        d_got = sb("d_got", [P, S], U32)
        d_codes = sb("d_codes", [P, S], U32)
        nc.vector.tensor_copy(d_got[:], d_word_tab[:].indirect(kidx_sb[:]))
        nc.vector.tensor_copy(
            d_codes[:].rearrange("p (t g i) -> p g t i", t=PACK, i=4),
            d_got[:].rearrange("p (g i t) -> p g t i", t=PACK, i=4),
        )
        x_codes = [sb("x_codes%d" % h, [P, HALF], U32) for h in range(2)]
        for h in range(2):
            nc.vector.tensor_copy(x_codes[h][:], x_word_tab[:].indirect(offs_sb[:, 16 * h : 16 * (h + 1)]))

        w1_rows = w1.rearrange("(p t) c -> p t c", t=PACK)
        w1_raw = [sb("w1_raw%d" % h, [P, PACK, HALF], F32, "slot_" + "eb"[h]) for h in range(2)]
        for h in range(2):
            nc.sync.dma_start(w1_raw[h][:], w1_rows[:, :, h * HALF : (h + 1) * HALF])
        w2_raw = sb("w2_raw", [P, PACK, S], F32, "slot_d")
        nc.sync.dma_start(w2_raw[:], w2.rearrange("(p t) c -> p t c", t=PACK))

        w1_bf = sb("w1_bf", [P, PACK, P, PACK], BF16, "slot_w")
        for h in range(2):
            nc.scalar.copy(
                w1_bf[:, :, 64 * h : 64 * (h + 1), :].rearrange("p u m t -> p m u t"),
                w1_raw[h][:].rearrange("p t (m u) -> p m u t", u=PACK),
            )
        w1_codes = sb("w1_codes", [P, S], U32)
        w1_scale = sb("w1_scale", [P, S], U8)

        s_bank = [psum.tile([P, PACK, CHUNK], F32, name="s_bank%d" % c, tag="a%d" % c) for c in range(CHUNKS)]
        for c in (0, 1, 3, 2):
            cols = slice(c % 2 * CHUNK, (c % 2 + 1) * CHUNK)
            for t in range(PACK):
                rows = slice(t * P, (t + 1) * P)
                mx(s_bank[c][:, t, :], d_codes[:, rows], d_scale[:, rows], x_codes[c // 2][:, cols],
                   x_scale[:, c * CHUNK : (c + 1) * CHUNK])
        z_planes = sb("z_planes", [P, PACK, CHUNK], BF16, "slot_b")
        for t in range(PACK):
            nc.scalar.activation(z_planes[:, t, :], s_bank[3][:, t, :], ACT.Copy, scale=gn16[:, t : t + 1])
        z_bf = [sb("z_bf%d" % h, [P, HALF, PACK], BF16) for h in range(2)]
        z_codes = [sb("z_codes%d" % h, [P, HALF], U32, "slot_y%d" % h) for h in range(2)]
        z_scale = [sb("z_scale%d" % h, [P, HALF], U8) for h in range(2)]
        gn_spread = gn16[:].unsqueeze(1).to_broadcast([P, CHUNK, PACK])

        def weigh(c):
            cols = slice(c % 2 * CHUNK, (c % 2 + 1) * CHUNK)
            nc.vector.tensor_tensor(
                z_bf[c // 2][:, cols, :], s_bank[c][:].rearrange("p t n -> p n t"), gn_spread, ALU.mult
            )

        def quantize_z(h):
            quantize(z_codes[h][:], z_scale[h][:], z_bf[h][:].rearrange("p n t -> p (n t)"))

        weigh(0)
        weigh(1)
        quantize(w1_codes[:], w1_scale[:], w1_bf[:].rearrange("p u m t -> p (u m t)"))
        quantize_z(0)
        nc.vector.tensor_copy(
            z_bf[1][:, CHUNK:HALF, :].rearrange("p (g i) t -> p g t i", i=4),
            z_planes[:].rearrange("p t (g i) -> p g t i", i=4),
        )
        weigh(2)
        quantize_z(1)

        res_sb = sb("res_sb", [P, 4, S], F32, "slot_b")
        nc.sync.dma_start(res_sb[:], res.rearrange("(m p) j -> p m j", p=P))

        h_own = [sb("h_own%d" % h, [P, PACK, HALF], F32) for h in range(2)]
        h_plane = [sb("h_plane%d" % u, [P, S], F32) for u in range(PACK)]
        h_bank = [
            [psum.tile([P, 2, HALF], F32, name="h_bank%d%d" % (h, b), tag="b%d%d" % (h, b)) for b in range(2)]
            for h in range(2)
        ]
        for h in range(2):
            for u in range(PACK):
                rows = slice(u * P, (u + 1) * P)
                mx(h_bank[h][u // 2][:, u % 2, :], w1_codes[:, rows], w1_scale[:, rows], z_codes[h][:], z_scale[h][:])
        for u in range(PACK):
            nc.scalar.activation(h_plane[u][:, 0:HALF], h_bank[0][u // 2][:, u % 2, :], ACT.Relu)
        nc.vector.tensor_scalar_max(h_own[0][:, 0:2, :], h_bank[0][0][:], 0.0)
        nc.vector.tensor_scalar_max(h_plane[0][:, HALF:S], h_bank[1][0][:, 0, :], 0.0)
        nc.scalar.activation(h_own[0][:, 2:4, :], h_bank[0][1][:], ACT.Relu)
        for u in range(1, PACK):
            nc.scalar.activation(h_plane[u][:, HALF:S], h_bank[1][u // 2][:, u % 2, :], ACT.Relu)
        for b in range(2):
            nc.scalar.activation(h_own[1][:, 2 * b : 2 * b + 2, :], h_bank[1][b][:], ACT.Relu)

        w2_bf = [sb("w2_bf%d" % h, [P, HALF, PACK], BF16, ("slot_w", "slot_y1")[h]) for h in range(2)]
        for c in range(CHUNKS):
            nc.scalar.copy(
                w2_bf[c // 2][:, c % 2 * CHUNK : (c % 2 + 1) * CHUNK, :].rearrange("p (c i) t -> p c t i", i=4),
                w2_raw[:, :, c * CHUNK : (c + 1) * CHUNK].rearrange("p t (c i) -> p c t i", i=4),
            )
        w2_codes = sb("w2_codes", [P, S], U32)
        w2_scale = sb("w2_scale", [P, S], U8)

        out_view = out.rearrange("(m p) j -> p m j", p=P)
        pieces = [(0, 256), (256, 384), (384, 512)]
        z2_bf, y_bank = {}, {}

        def join(k, slot=None):
            first, last = pieces[k]
            width = last - first
            z2 = sb("z2_%d" % k, [P, PACK, width], F32, slot)
            own = h_own[first // HALF][:, :, first % HALF : first % HALF + width]
            for u in range(PACK):
                picked = h_plane[u][:].indirect(nb_sb[:, first // 16 : last // 16])
                nc.vector.tensor_tensor(z2[:, u, :], picked, own[:, u, :], ALU.add)
            z2_bf[k] = sb("z2_bf%d" % k, [P, width, PACK], BF16, "slot_z%d" % k)
            nc.scalar.copy(
                z2_bf[k][:].rearrange("p (g i) u -> p g u i", i=4), z2[:].rearrange("p u (g i) -> p g u i", i=4)
            )

        def last_layer(k):
            first, last = pieces[k]
            width = last - first
            codes = sb("z2_codes%d" % k, [P, width], U32)
            scale = sb("z2_scale%d" % k, [P, width], U8)
            quantize(codes[:], scale[:], z2_bf[k][:].rearrange("p n t -> p (n t)"))
            per_bank = S // width
            for b in range(4 // per_bank):
                tag = "a%d" % (first // CHUNK + b)
                y_bank[k, b] = psum.tile([P, per_bank, width], F32, name="y_bank%d%d" % (k, b), tag=tag)
                for i in range(per_bank):
                    rows = slice((b * per_bank + i) * P, (b * per_bank + i + 1) * P)
                    mx(y_bank[k, b][:, i, :], w2_codes[:, rows], w2_scale[:, rows], codes[:], scale[:])

        def finish(k, b):
            first, last = pieces[k]
            width = last - first
            per_bank = S // width
            half = per_bank // 2
            y = sb("y%d%d" % (k, b), [P, per_bank, width], F32)
            lo = b * per_bank
            nc.vector.tensor_tensor(y[:], y_bank[k, b][:], res_sb[:, lo : lo + per_bank, first:last], ALU.add)
            nc.sync.dma_start(out_view[:, lo : lo + half, first:last], y[:, 0:half, :])
            nc.scalar.dma_start(out_view[:, lo + half : lo + per_bank, first:last], y[:, half:per_bank, :])

        join(0)
        join(1)
        for h in range(2):
            cols = slice(h * HALF, (h + 1) * HALF)
            quantize(w2_codes[:, cols], w2_scale[:, cols], w2_bf[h][:].rearrange("p c t -> p (c t)"))
        last_layer(0)
        join(2, "slot_z0")
        last_layer(1)
        finish(0, 0)
        last_layer(2)
        finish(0, 1)
        finish(1, 0)
        finish(2, 0)
